import numpy as np
import ml_dtypes


def mxq(x, axis, fmt="e4m3"):
    dtype, down = {"e4m3": (ml_dtypes.float8_e4m3fn, 7), "e5m2": (ml_dtypes.float8_e5m2, 14)}[fmt]
    v = np.moveaxis(np.asarray(x, np.float32).astype(ml_dtypes.bfloat16).astype(np.float64), axis, -1)
    blocks = v.reshape(v.shape[:-1] + (-1, 32))
    amax = np.abs(blocks).max(-1, keepdims=True)
    byte = np.maximum(np.where(amax > 0, np.frexp(amax)[1] - 1 + 127, 0) - down, 1)
    scale = np.exp2(byte - 127.0)
    codes = (blocks / scale).astype(np.float32).astype(dtype).astype(np.float64)
    return np.moveaxis((codes * scale).reshape(v.shape), -1, axis)


WIDE = False


def mx_kscale(k):
    if not WIDE:
        return np.ones(k)
    levels = np.array([10, -10, 5, -5, 0])
    if k % 512:
        return np.exp2(np.random.permutation(np.resize(levels, k // 32))).repeat(32)
    a = np.empty((k // 512, 16))
    for p in range(k // 512):
        a[p, :8] = np.random.permutation(np.resize(levels, 8))
        for g in range(8):
            far = levels[np.abs(levels - a[p, g]) >= 10]
            a[p, g + 8] = far[np.random.randint(len(far))]
    return np.exp2(a.ravel()).repeat(32)


BF16 = ml_dtypes.bfloat16


def bf(x):
    return np.asarray(x, np.float32).astype(BF16)


def f64(x):
    return np.asarray(x).astype(np.float64)


E2M1 = np.array([0.0, 0.5, 1.0, 1.5, 2.0, 3.0, 4.0, 6.0, -0.0, -0.5, -1.0, -1.5, -2.0, -3.0, -4.0, -6.0])


def pack_weight(w, fmt):
    k, n = w.shape
    w = f64(bf(w)).reshape(k // 32, 32, n)
    amax = np.abs(w).max(1)
    if fmt == "e4m3":
        byte = np.frexp(amax)[1] - 1 + 127 - 7
    else:
        mant, ex = np.frexp(amax / 6.0)
        byte = np.where(mant > 0.5, ex, ex - 1) + 127
    byte = np.clip(np.where(amax > 0, byte, 1), 1, 254)
    scaled = (w * np.exp2(127.0 - byte)[:, None, :]).reshape(k, n).astype(np.float32)
    by_word = np.ascontiguousarray(scaled.reshape(k // 512, 128, 4, n).transpose(0, 1, 3, 2))
    if fmt == "e4m3":
        words = by_word.astype(ml_dtypes.float8_e4m3fn).view(np.uint8)
    else:
        c = by_word.astype(ml_dtypes.float4_e2m1fn).view(np.uint8) & 0xF
        words = c[..., 0::2] | (c[..., 1::2] << 4)
    return np.ascontiguousarray(words), np.ascontiguousarray(byte.astype(np.uint8).reshape(k // 512, 16, n))


def unpack_weight(words, scales, fmt):
    g, p, n, _ = words.shape
    if fmt == "e4m3":
        vals = np.ascontiguousarray(words).view(ml_dtypes.float8_e4m3fn).astype(np.float64)
    else:
        nib = np.empty((g, p, n, 4), np.uint8)
        nib[..., 0::2] = words & 0xF
        nib[..., 1::2] = words >> 4
        vals = E2M1[nib]
    vals = vals * np.repeat(np.exp2(scales.astype(np.float64) - 127.0), 8, axis=1)[..., None]
    return vals.transpose(0, 1, 3, 2).reshape(g * 512, n)
def pack4(w):
    words, scales = pack_weight(w, "e2m1")
    return words.reshape(words.shape[0], 128, -1), scales


def unpack4(words, scales):
    return unpack_weight(words.reshape(words.shape[0], 128, -1, 2), scales, "e2m1")


def planes(Y):
    n, m = Y.shape
    b = f64(bf(Y)).reshape(n // 32, 32, m)
    amax = np.abs(b).max(1)
    byte = np.clip(np.where(amax > 0, np.frexp(amax)[1] - 1 + 127 - 7, 1), 1, 254)
    codes = (b * np.exp2(127.0 - byte)[:, None, :]).reshape(n, m).astype(np.float32).astype(ml_dtypes.float8_e4m3fn).view(np.uint8)
    words = codes.reshape(n // 512, 128, 4, m).transpose(0, 1, 3, 2)
    return np.ascontiguousarray(words), np.ascontiguousarray(byte.astype(np.uint8).reshape(n // 512, 16, m))


N, M = 1024, 1536
LAN, CLEAN, MAIL = 0.6, 0.35, 0.5

def coupling(strength, h):
    return strength * 0.5 * np.random.randn(N, N) * h[None, :] / np.sqrt(N)

def setup_inputs():
    t = mx_kscale(N)
    h = np.exp(0.7 * np.random.randn(N))
    x = 0.5 * h[:, None] * np.random.randn(N, M)
    A = coupling(LAN, h)
    C = coupling(CLEAN, h)
    B = coupling(MAIL, h)
    B_words, B_scales = pack4(B / t[:, None])
    S = 0.3 + 0.6 * np.random.rand(N, M)
    keep = 0.7 + 0.2 * np.random.rand(N)
    return {"x": bf(x * t[:, None]),
            "A": bf(A * t[None, :] / t[:, None]),
            "C": bf(C * t[None, :] / t[:, None]),
            "B_words": B_words, "B_scales": B_scales,
            "S": bf(S), "keep": bf(keep / t)}

def reference(x, A, C, B_words, B_scales, S, keep):
    x, A, C, S, keep = f64(x), f64(A), f64(C), f64(S), f64(keep)
    B = unpack4(B_words, B_scales)
    x1 = x + S * (mxq(A, 0, "e4m3").T @ mxq(x, 0, "e4m3"))
    x2 = x1 - (mxq(C, 0, "e4m3").T @ mxq(x1, 0, "e4m3"))
    y = keep[:, None] * x2 + S * (B.T @ mxq(x2, 0, "e4m3"))
    Y = y
    words, scales = planes(Y)
    return y, words, scales

@@ -1,0 +1,326 @@
+from contextlib import ExitStack
+
+import concourse.mybir as mybir
+
+N, M = 1024, 1536
+FLOPS = 3 * 2 * N * N * M
+
+F32 = mybir.dt.float32
+BF16 = mybir.dt.bfloat16
+I32 = mybir.dt.int32
+U32 = mybir.dt.uint32
+U8 = mybir.dt.uint8
+FP8X4 = mybir.dt.float8_e4m3fn_x4
+FP4X4 = mybir.dt.float4_e2m1fn_x4
+ALU = mybir.AluOpType
+
+P = 128
+PACK = 4
+GROUP = P * PACK
+GROUPS = N // GROUP
+BANK = 512
+FP4_N = 128
+
+CHUNKS = [(0, 128), (128, 384), (384, 640), (640, 896), (896, 1152), (1152, 1408), (1408, 1536)]
+BLOCKS = [(0, 128), (128, 384), (384, 896), (896, 1536)]
+
+
+def tile_malware_excess_rounds_k1_kernel(tc, x, A, C, B_words, B_scales, S, keep, out_0, out_1, out_2):
+    nc = tc.nc
+    with ExitStack() as ctx:
+        hold = ctx.enter_context(tc.tile_pool(name="hold", bufs=1))
+        work = ctx.enter_context(tc.tile_pool(name="work", bufs=2))
+        psum = ctx.enter_context(tc.psum_pool(name="psum", bufs=8))
+        ctx.enter_context(tc.manual_schedule())
+
+        def load_rows(src, name, g, lo, hi):
+            raw = hold.tile([P, PACK, hi - lo], BF16, name=name, align_bytes=64)
+            rows = src[g * GROUP:(g + 1) * GROUP, lo:hi]
+            nc.sync.dma_start(out=raw[:], in_=rows.rearrange("(p t) m -> p t m", t=PACK))
+            return raw
+
+        raw_x, raw_s, raw_w = {}, {}, {}
+
+        def load_block(store, src, label, b):
+            for g in range(GROUPS):
+                store[b, g] = load_rows(src, "%s%d_%d" % (label, b, g), g, *BLOCKS[b])
+
+        def load_weight(src, label, h):
+            for g in range(GROUPS):
+                raw_w[label, g, h] = load_rows(src, "%s%d_%d" % (label, g, h), g, h * GROUP, (h + 1) * GROUP)
+
+        def chunk_of(store, c, g):
+            lo, hi = CHUNKS[c]
+            b = max(i for i in range(len(BLOCKS)) if BLOCKS[i][0] <= lo)
+            return store[b, g][:, :, lo - BLOCKS[b][0]:hi - BLOCKS[b][0]]
+
+        b_scale_raw = hold.tile([P, GROUPS, N], U8, align_bytes=64)
+        nc.gpsimd.memset(b_scale_raw[:].bitcast(I32), 0)
+
+        def load_weight_piece(src, label, g, h):
+            raw_w[label, g, h] = load_rows(src, "%s%d_%d" % (label, g, h), g, h * GROUP, (h + 1) * GROUP)
+
+        def load_half(store, src, label, b, g):
+            store[b, g] = load_rows(src, "%s%d_%d" % (label, b, g), g, *BLOCKS[b])
+
+        def load_weight_rows(src, label, g):
+            raw = load_rows(src, "%s%d" % (label, g), g, 0, N)
+            for h in range(GROUPS):
+                raw_w[label, g, h] = raw[:, :, h * GROUP:(h + 1) * GROUP]
+
+        keep_raw = hold.tile([P, GROUPS, PACK], BF16, align_bytes=64)
+        load_weight_piece(A, "A", 0, 0)
+        load_block(raw_x, x, "x", 0)
+        load_weight_rows(A, "A", 1)
+        load_half(raw_s, S, "s", 0, 0)
+        load_weight_piece(A, "A", 0, 1)
+        load_half(raw_s, S, "s", 0, 1)
+        load_block(raw_x, x, "x", 1)
+        b_word_raw = hold.tile([P, GROUPS, 2 * N], U8, align_bytes=64)
+        nc.sync.dma_start(out=b_word_raw[:].bitcast(I32), in_=B_words.rearrange("g p n -> p g n").bitcast(I32))
+        for q in range(4):
+            nc.sync.dma_start(
+                out=b_scale_raw[32 * q:32 * q + 4, :, :].bitcast(I32),
+                in_=B_scales[:, 4 * q:4 * q + 4, :].rearrange("g r n -> r g n").bitcast(I32),
+            )
+        load_weight_rows(C, "C", 0)
+        load_weight_rows(C, "C", 1)
+        load_block(raw_s, S, "s", 1)
+        nc.sync.dma_start(out=keep_raw[:], in_=keep.rearrange("(g p t) -> p g t", g=GROUPS, t=PACK))
+        for b in range(2, len(BLOCKS)):
+            load_block(raw_x, x, "x", b)
+            load_block(raw_s, S, "s", b)
+
+        grouped_w, weights = {}, {}
+
+        def group_weight(copy, label, g, h):
+            grouped = work.tile([P, GROUP * PACK], BF16, name="grouped_w", bufs=3, align_bytes=64)
+            copy(
+                out=grouped[:].rearrange("p (t c i j) -> p c t i j", t=PACK, i=2, j=PACK),
+                in_=raw_w[label, g, h][:, :, :].rearrange("p j (c i t) -> p c t i j", i=2, t=PACK),
+            )
+            grouped_w[label, g, h] = grouped
+
+        def quantize_weight(label, g, h):
+            codes = hold.tile([P, GROUP], U32, name="%s_codes%d_%d" % (label, g, h), align_bytes=64)
+            scales = hold.tile([P, GROUP], U8, name="%s_scales%d_%d" % (label, g, h), align_bytes=64)
+            nc.vector.quantize_mx(out=codes[:].bitcast(FP8X4), scales=scales[:], in_=grouped_w[label, g, h][:])
+            for t in range(PACK):
+                cols = slice(t * P, (t + 1) * P)
+                weights[label, g, h, t] = (codes[:, cols].bitcast(FP8X4), scales[:, cols])
+
+        def reorder_b(h):
+            for g in range(GROUPS):
+                words = hold.tile([P, 2 * GROUP], U8, name="B_codes%d_%d" % (g, h), align_bytes=64)
+                nc.vector.tensor_copy(
+                    out=words[:].rearrange("p (t c i b) -> p c t i b", t=PACK, i=8, b=2),
+                    in_=b_word_raw[:, g, 2 * GROUP * h:2 * GROUP * (h + 1)].rearrange("p (c i t b) -> p c t i b", i=8, t=PACK, b=2),
+                )
+                scales = hold.tile([P, GROUP], U8, name="B_scales%d_%d" % (g, h), align_bytes=64)
+                nc.vector.tensor_copy(
+                    out=scales[:].rearrange("p (t c i) -> p c t i", t=PACK, i=16),
+                    in_=b_scale_raw[:, g, GROUP * h:GROUP * (h + 1)].rearrange("p (c i t) -> p c t i", i=16, t=PACK),
+                )
+                for t in range(PACK):
+                    weights["B", g, h, t] = (
+                        words[:, 2 * P * t:2 * P * (t + 1)].bitcast(FP4X4),
+                        scales[:, P * t:P * (t + 1)],
+                    )
+
+        grouped_a, acts, state, result = {}, {}, {}, {}
+        y_scales = hold.tile([P, GROUPS, M], U8, align_bytes=64)
+
+        def width(c):
+            return CHUNKS[c][1] - CHUNKS[c][0]
+
+        def group_act(label, c, g, src):
+            grouped = work.tile([P, width(c), PACK], BF16, name="grouped_%s%d" % (label, g), align_bytes=64)
+            nc.scalar.copy(
+                out=grouped[:].rearrange("p (c i) t -> p c t i", i=4),
+                in_=src.rearrange("p t (c i) -> p c t i", i=4),
+            )
+            grouped_a[label, c, g] = grouped
+
+        def quantize_act(label, c, g):
+            codes = work.tile([P, width(c)], U32, name="codes_%s%d" % (label, g), align_bytes=64)
+            scales = work.tile([P, width(c)], U8, name="scales_%s%d" % (label, g), align_bytes=64)
+            nc.vector.quantize_mx(
+                out=codes[:].bitcast(FP8X4), scales=scales[:], in_=grouped_a[label, c, g][:].rearrange("p m t -> p (m t)")
+            )
+            acts[label, c, g] = (codes, scales)
+
+        def quantize_result(c, g):
+            lo, hi = CHUNKS[c]
+            codes = work.tile([P, width(c)], U32, name="codes_y%d" % g, align_bytes=64)
+            nc.vector.quantize_mx(
+                out=codes[:].bitcast(FP8X4), scales=y_scales[:, g, lo:hi], in_=grouped_a["y", c, g][:].rearrange("p m t -> p (m t)")
+            )
+            nc.sync.dma_start(
+                out=out_1[g, :, lo:hi, :].rearrange("p m t -> p (m t)").bitcast(I32), in_=codes[:].bitcast(I32)
+            )
+
+        def store_scales(lo, hi):
+            for q in range(4):
+                nc.sync.dma_start(
+                    out=out_2[:, 4 * q:4 * q + 4, lo:hi].rearrange("g r m -> r g m").bitcast(I32),
+                    in_=y_scales[32 * q:32 * q + 4, :, lo:hi].bitcast(I32),
+                )
+
+        def product(w_label, a_label, c, h, drain):
+            w = width(c)
+            per_bank = BANK // w
+            n = FP4_N if w_label == "B" else w
+            for t0 in range(0, PACK, per_bank):
+                bank = psum.tile([P, per_bank, w], F32, name="bank")
+                for t in range(t0, t0 + per_bank):
+                    for m0 in range(0, w, n):
+                        for g in range(GROUPS):
+                            codes, scales = acts[a_label, c, g]
+                            nc.tensor.matmul_mx(
+                                out=bank[:, t - t0, m0:m0 + n],
+                                lhsT=weights[w_label, g, h, t][0],
+                                lhsT_scale=weights[w_label, g, h, t][1],
+                                rhs=codes[:, m0:m0 + n].bitcast(FP8X4),
+                                rhs_scale=scales[:, m0:m0 + n],
+                                start=(g == 0),
+                                stop=(g == GROUPS - 1),
+                            )
+                drain(bank, slice(t0, t0 + per_bank))
+
+        def round_one(c, h):
+            x1 = work.tile([P, PACK, width(c)], F32, name="state%d" % h, bufs=3, align_bytes=64)
+            gate = chunk_of(raw_s, c, h)
+            product("A", "x", c, h, lambda bank, ts: nc.vector.tensor_tensor(out=x1[:, ts, :], in0=bank[:], in1=gate[:, ts, :], op=ALU.mult))
+            state[c, h] = x1
+
+        def add_x(engine, c, h):
+            x1 = state[c, h]
+            engine.tensor_tensor(out=x1[:], in0=x1[:], in1=chunk_of(raw_x, c, h), op=ALU.add)
+
+        def round_two(c, h):
+            x2 = state[c, h]
+            product("C", "x1", c, h, lambda bank, ts: nc.vector.tensor_tensor(out=x2[:, ts, :], in0=x2[:, ts, :], in1=bank[:], op=ALU.subtract))
+
+        def round_three(c, h):
+            y = work.tile([P, PACK, width(c)], F32, name="result%d" % h, align_bytes=64)
+            gate = chunk_of(raw_s, c, h)
+            product("B", "x2", c, h, lambda bank, ts: nc.vector.tensor_tensor(out=y[:, ts, :], in0=bank[:], in1=gate[:, ts, :], op=ALU.mult))
+            result[c, h] = y
+
+        def recover(c, h):
+            lo, hi = CHUNKS[c]
+            y = result[c, h]
+            for t in range(PACK):
+                nc.vector.scalar_tensor_tensor(
+                    out=y[:, t, :], in0=state[c, h][:, t, :], scalar=keep_raw[:, h, t:t + 1], in1=y[:, t, :],
+                    op0=ALU.mult, op1=ALU.add,
+                )
+            nc.sync.dma_start(out=out_0[h * GROUP:(h + 1) * GROUP, lo:hi].rearrange("(p t) m -> p t m", t=PACK), in_=y[:])
+
+        def group_x(c):
+            for g in range(GROUPS):
+                group_act("x", c, g, chunk_of(raw_x, c, g))
+
+        def quantize_both(label, c):
+            for g in range(GROUPS):
+                quantize_act(label, c, g)
+
+        def finish(c, h):
+            recover(c, h)
+            group_act("y", c, h, result[c, h][:])
+
+        on_vector, on_scalar = nc.vector.tensor_copy, nc.scalar.copy
+
+        group_weight(on_vector, "A", 0, 0)
+        group_x(0)
+        quantize_weight("A", 0, 0)
+        quantize_both("x", 0)
+        group_weight(on_vector, "A", 1, 0)
+        group_weight(on_scalar, "A", 1, 1)
+        quantize_weight("A", 1, 0)
+        group_weight(on_scalar, "A", 0, 1)
+        quantize_weight("A", 1, 1)
+        round_one(0, 0)
+        quantize_weight("A", 0, 1)
+        group_x(1)
+        add_x(nc.vector, 0, 0)
+        group_act("x1", 0, 0, state[0, 0][:])
+        group_weight(on_scalar, "C", 0, 0)
+        reorder_b(0)
+        round_one(0, 1)
+        quantize_both("x", 1)
+        add_x(nc.vector, 0, 1)
+        group_act("x1", 0, 1, state[0, 1][:])
+        group_weight(on_scalar, "C", 0, 1)
+        reorder_b(1)
+        quantize_weight("C", 0, 0)
+        quantize_both("x1", 0)
+        group_weight(on_scalar, "C", 1, 0)
+        group_x(2)
+        group_weight(on_vector, "C", 1, 1)
+        quantize_weight("C", 0, 1)
+        round_one(1, 0)
+        quantize_weight("C", 1, 1)
+        quantize_weight("C", 1, 0)
+        add_x(nc.vector, 1, 0)
+        group_act("x1", 1, 0, state[1, 0][:])
+        round_one(1, 1)
+        round_two(0, 0)
+        add_x(nc.vector, 1, 1)
+        group_act("x1", 1, 1, state[1, 1][:])
+        round_two(0, 1)
+        for h in range(GROUPS):
+            group_act("x2", 0, h, state[0, h][:])
+        quantize_both("x", 2)
+        quantize_both("x1", 1)
+        quantize_both("x2", 0)
+
+        last = len(CHUNKS) - 1
+        for step in range(2, last + 1):
+            first, second, third, fourth, ahead = step, step - 1, step - 2, step - 3, step + 1
+            if ahead <= last:
+                group_x(ahead)
+            for h in range(GROUPS):
+                round_one(first, h)
+                add_x(nc.gpsimd, first, h)
+            for h in range(GROUPS):
+                round_two(second, h)
+            for h in range(GROUPS):
+                group_act("x1", first, h, state[first, h][:])
+                group_act("x2", second, h, state[second, h][:])
+            for h in range(GROUPS):
+                round_three(third, h)
+            if ahead <= last:
+                quantize_both("x", ahead)
+            for h in range(GROUPS):
+                finish(third, h)
+            if fourth >= 0:
+                for g in range(GROUPS):
+                    quantize_result(fourth, g)
+            if step < last:
+                quantize_both("x1", first)
+                quantize_both("x2", second)
+            else:
+                quantize_both("x2", second)
+                quantize_both("x1", first)
+
+        for g in range(GROUPS):
+            quantize_result(last - 2, g)
+        store_scales(0, CHUNKS[last - 2][1])
+        round_three(last - 1, 0)
+        for h in range(GROUPS):
+            round_two(last, h)
+            group_act("x2", last, h, state[last, h][:])
+        round_three(last - 1, 1)
+        quantize_both("x2", last)
+        for h in range(GROUPS):
+            finish(last - 1, h)
+        round_three(last, 0)
+        round_three(last, 1)
+        finish(last, 0)
+        quantize_result(last - 1, 0)
+        finish(last, 1)
+        quantize_result(last - 1, 1)
+        for g in range(GROUPS):
+            quantize_result(last, g)
+        store_scales(CHUNKS[last - 1][0], M)

@@ -20,6 +20,7 @@ GROUP = P * PACK
 GROUPS = N // GROUP
 BANK = 512
 FP4_N = 128
+SPLIT = True
 
 CHUNKS = [(0, 128), (128, 384), (384, 640), (640, 896), (896, 1152), (1152, 1408), (1408, 1536)]
 BLOCKS = [(0, 128), (128, 384), (384, 896), (896, 1536)]
@@ -54,9 +55,6 @@ def tile_malware_excess_rounds_k1_kernel(tc, x, A, C, B_words, B_scales, S, keep
             b = max(i for i in range(len(BLOCKS)) if BLOCKS[i][0] <= lo)
             return store[b, g][:, :, lo - BLOCKS[b][0]:hi - BLOCKS[b][0]]
 
-        b_scale_raw = hold.tile([P, GROUPS, N], U8, align_bytes=64)
-        nc.gpsimd.memset(b_scale_raw[:].bitcast(I32), 0)
-
         def load_weight_piece(src, label, g, h):
             raw_w[label, g, h] = load_rows(src, "%s%d_%d" % (label, g, h), g, h * GROUP, (h + 1) * GROUP)
 
@@ -69,13 +67,8 @@ def tile_malware_excess_rounds_k1_kernel(tc, x, A, C, B_words, B_scales, S, keep
                 raw_w[label, g, h] = raw[:, :, h * GROUP:(h + 1) * GROUP]
 
         keep_raw = hold.tile([P, GROUPS, PACK], BF16, align_bytes=64)
-        load_weight_piece(A, "A", 0, 0)
-        load_block(raw_x, x, "x", 0)
-        load_weight_rows(A, "A", 1)
-        load_half(raw_s, S, "s", 0, 0)
-        load_weight_piece(A, "A", 0, 1)
-        load_half(raw_s, S, "s", 0, 1)
-        load_block(raw_x, x, "x", 1)
+        b_scale_raw = hold.tile([P, GROUPS, N], U8, align_bytes=64)
+        nc.vector.memset(b_scale_raw[:].bitcast(I32), 0)
         b_word_raw = hold.tile([P, GROUPS, 2 * N], U8, align_bytes=64)
         nc.sync.dma_start(out=b_word_raw[:].bitcast(I32), in_=B_words.rearrange("g p n -> p g n").bitcast(I32))
         for q in range(4):
@@ -83,10 +76,15 @@ def tile_malware_excess_rounds_k1_kernel(tc, x, A, C, B_words, B_scales, S, keep
                 out=b_scale_raw[32 * q:32 * q + 4, :, :].bitcast(I32),
                 in_=B_scales[:, 4 * q:4 * q + 4, :].rearrange("g r n -> r g n").bitcast(I32),
             )
-        load_weight_rows(C, "C", 0)
-        load_weight_rows(C, "C", 1)
-        load_block(raw_s, S, "s", 1)
+        load_block(raw_x, x, "x", 0)
+        load_weight_rows(A, "A", 0)
+        load_weight_rows(A, "A", 1)
+        load_block(raw_s, S, "s", 0)
         nc.sync.dma_start(out=keep_raw[:], in_=keep.rearrange("(g p t) -> p g t", g=GROUPS, t=PACK))
+        load_block(raw_x, x, "x", 1)
+        load_weight_rows(C, "C", 0)
+        load_block(raw_s, S, "s", 1)
+        load_weight_rows(C, "C", 1)
         for b in range(2, len(BLOCKS)):
             load_block(raw_x, x, "x", b)
             load_block(raw_s, S, "s", b)
@@ -94,7 +92,7 @@ def tile_malware_excess_rounds_k1_kernel(tc, x, A, C, B_words, B_scales, S, keep
         grouped_w, weights = {}, {}
 
         def group_weight(copy, label, g, h):
-            grouped = work.tile([P, GROUP * PACK], BF16, name="grouped_w", bufs=3, align_bytes=64)
+            grouped = work.tile([P, GROUP * PACK], BF16, name="grouped_w", bufs=4, align_bytes=64)
             copy(
                 out=grouped[:].rearrange("p (t c i j) -> p c t i j", t=PACK, i=2, j=PACK),
                 in_=raw_w[label, g, h][:, :, :].rearrange("p j (c i t) -> p c t i j", i=2, t=PACK),
@@ -109,23 +107,30 @@ def tile_malware_excess_rounds_k1_kernel(tc, x, A, C, B_words, B_scales, S, keep
                 cols = slice(t * P, (t + 1) * P)
                 weights[label, g, h, t] = (codes[:, cols].bitcast(FP8X4), scales[:, cols])
 
-        def reorder_b(h):
+        b_scales = {}
+
+        def reorder_b_words(h):
             for g in range(GROUPS):
                 words = hold.tile([P, 2 * GROUP], U8, name="B_codes%d_%d" % (g, h), align_bytes=64)
                 nc.vector.tensor_copy(
                     out=words[:].rearrange("p (t c i b) -> p c t i b", t=PACK, i=8, b=2),
                     in_=b_word_raw[:, g, 2 * GROUP * h:2 * GROUP * (h + 1)].rearrange("p (c i t b) -> p c t i b", i=8, t=PACK, b=2),
                 )
-                scales = hold.tile([P, GROUP], U8, name="B_scales%d_%d" % (g, h), align_bytes=64)
-                nc.vector.tensor_copy(
-                    out=scales[:].rearrange("p (t c i) -> p c t i", t=PACK, i=16),
-                    in_=b_scale_raw[:, g, GROUP * h:GROUP * (h + 1)].rearrange("p (c i t) -> p c t i", i=16, t=PACK),
-                )
+                scales = b_scales[g, h]
                 for t in range(PACK):
                     weights["B", g, h, t] = (
                         words[:, 2 * P * t:2 * P * (t + 1)].bitcast(FP4X4),
                         scales[:, P * t:P * (t + 1)],
                     )
+
+        def reorder_b_scales(h):
+            for g in range(GROUPS):
+                scales = hold.tile([P, GROUP], U8, name="B_scales%d_%d" % (g, h), align_bytes=64)
+                nc.vector.tensor_copy(
+                    out=scales[:].rearrange("p (t c i) -> p c t i", t=PACK, i=16),
+                    in_=b_scale_raw[:, g, GROUP * h:GROUP * (h + 1)].rearrange("p (c i t) -> p c t i", i=16, t=PACK),
+                )
+                b_scales[g, h] = scales
 
         grouped_a, acts, state, result = {}, {}, {}, {}
         y_scales = hold.tile([P, GROUPS, M], U8, align_bytes=64)
@@ -133,9 +138,9 @@ def tile_malware_excess_rounds_k1_kernel(tc, x, A, C, B_words, B_scales, S, keep
         def width(c):
             return CHUNKS[c][1] - CHUNKS[c][0]
 
-        def group_act(label, c, g, src):
+        def group_act(label, c, g, src, copy=nc.scalar.copy):
             grouped = work.tile([P, width(c), PACK], BF16, name="grouped_%s%d" % (label, g), align_bytes=64)
-            nc.scalar.copy(
+            copy(
                 out=grouped[:].rearrange("p (c i) t -> p c t i", i=4),
                 in_=src.rearrange("p t (c i) -> p c t i", i=4),
             )
@@ -149,14 +154,16 @@ def tile_malware_excess_rounds_k1_kernel(tc, x, A, C, B_words, B_scales, S, keep
             )
             acts[label, c, g] = (codes, scales)
 
-        def quantize_result(c, g):
+        def quantize_result(c):
             lo, hi = CHUNKS[c]
-            codes = work.tile([P, width(c)], U32, name="codes_y%d" % g, align_bytes=64)
-            nc.vector.quantize_mx(
-                out=codes[:].bitcast(FP8X4), scales=y_scales[:, g, lo:hi], in_=grouped_a["y", c, g][:].rearrange("p m t -> p (m t)")
-            )
+            codes = work.tile([P, GROUPS, width(c)], U32, name="codes_y", bufs=3, align_bytes=64)
+            for g in range(GROUPS):
+                nc.vector.quantize_mx(
+                    out=codes[:, g, :].bitcast(FP8X4), scales=y_scales[:, g, lo:hi],
+                    in_=grouped_a["y", c, g][:].rearrange("p m t -> p (m t)"),
+                )
             nc.sync.dma_start(
-                out=out_1[g, :, lo:hi, :].rearrange("p m t -> p (m t)").bitcast(I32), in_=codes[:].bitcast(I32)
+                out=out_1[:, :, lo:hi, :].rearrange("g p m t -> p g (m t)").bitcast(I32), in_=codes[:].bitcast(I32)
             )
 
         def store_scales(lo, hi):
@@ -166,11 +173,13 @@ def tile_malware_excess_rounds_k1_kernel(tc, x, A, C, B_words, B_scales, S, keep
                     in_=y_scales[32 * q:32 * q + 4, :, lo:hi].bitcast(I32),
                 )
 
-        def product(w_label, a_label, c, h, drain):
+        filled = {}
+
+        def multiply(w_label, a_label, c, h, slots=range(PACK)):
             w = width(c)
             per_bank = BANK // w
             n = FP4_N if w_label == "B" else w
-            for t0 in range(0, PACK, per_bank):
+            for t0 in slots[::per_bank]:
                 bank = psum.tile([P, per_bank, w], F32, name="bank")
                 for t in range(t0, t0 + per_bank):
                     for m0 in range(0, w, n):
@@ -185,37 +194,58 @@ def tile_malware_excess_rounds_k1_kernel(tc, x, A, C, B_words, B_scales, S, keep
                                 start=(g == 0),
                                 stop=(g == GROUPS - 1),
                             )
-                drain(bank, slice(t0, t0 + per_bank))
+                filled[w_label, c, h, t0] = bank
 
-        def round_one(c, h):
+        def banks_of(w_label, c, h, slots=range(PACK)):
+            per_bank = BANK // width(c)
+            return [(filled[w_label, c, h, t0], slice(t0, t0 + per_bank)) for t0 in slots[::per_bank]]
+
+        def gate_one(c, h):
             x1 = work.tile([P, PACK, width(c)], F32, name="state%d" % h, bufs=3, align_bytes=64)
-            gate = chunk_of(raw_s, c, h)
-            product("A", "x", c, h, lambda bank, ts: nc.vector.tensor_tensor(out=x1[:, ts, :], in0=bank[:], in1=gate[:, ts, :], op=ALU.mult))
+            for bank, ts in banks_of("A", c, h):
+                nc.vector.tensor_tensor(out=x1[:, ts, :], in0=bank[:], in1=chunk_of(raw_s, c, h)[:, ts, :], op=ALU.mult)
             state[c, h] = x1
 
         def add_x(engine, c, h):
             x1 = state[c, h]
             engine.tensor_tensor(out=x1[:], in0=x1[:], in1=chunk_of(raw_x, c, h), op=ALU.add)
 
-        def round_two(c, h):
+        def subtract_two(c, h):
             x2 = state[c, h]
-            product("C", "x1", c, h, lambda bank, ts: nc.vector.tensor_tensor(out=x2[:, ts, :], in0=x2[:, ts, :], in1=bank[:], op=ALU.subtract))
+            for bank, ts in banks_of("C", c, h):
+                nc.vector.tensor_tensor(out=x2[:, ts, :], in0=x2[:, ts, :], in1=bank[:], op=ALU.subtract)
 
-        def round_three(c, h):
-            y = work.tile([P, PACK, width(c)], F32, name="result%d" % h, align_bytes=64)
-            gate = chunk_of(raw_s, c, h)
-            product("B", "x2", c, h, lambda bank, ts: nc.vector.tensor_tensor(out=y[:, ts, :], in0=bank[:], in1=gate[:, ts, :], op=ALU.mult))
-            result[c, h] = y
-
-        def recover(c, h):
-            lo, hi = CHUNKS[c]
+        def gate_three(c, h, slots=range(PACK)):
+            if (c, h) not in result:
+                y = work.tile([P, PACK, width(c)], F32, name="result%d" % h, align_bytes=64)
+                result[c, h] = y
             y = result[c, h]
-            for t in range(PACK):
+            for bank, ts in banks_of("B", c, h, slots):
+                nc.vector.tensor_tensor(out=y[:, ts, :], in0=bank[:], in1=chunk_of(raw_s, c, h)[:, ts, :], op=ALU.mult)
+
+        def recover(c, h, slots):
+            y = result[c, h]
+            for t in slots:
                 nc.vector.scalar_tensor_tensor(
-                    out=y[:, t, :], in0=state[c, h][:, t, :], scalar=keep_raw[:, h, t:t + 1], in1=y[:, t, :],
+                    out=y[:, t, :], in0=state[c, h][:, t, :], scalar=keep_f32[:, h, t:t + 1], in1=y[:, t, :],
                     op0=ALU.mult, op1=ALU.add,
                 )
-            nc.sync.dma_start(out=out_0[h * GROUP:(h + 1) * GROUP, lo:hi].rearrange("(p t) m -> p t m", t=PACK), in_=y[:])
+
+        def scale_by_keep(c, h, slots):
+            for t in slots:
+                x2 = state[c, h][:, t, :]
+                nc.scalar.activation(out=x2, in_=x2, func=mybir.ActivationFunctionType.Copy, scale=keep_f32[:, h, t:t + 1])
+
+        def add_kept(c, h, slots):
+            ts = slice(slots.start, slots.stop)
+            y = result[c, h][:, ts, :]
+            nc.gpsimd.tensor_tensor(out=y, in0=y, in1=state[c, h][:, ts, :], op=ALU.add)
+
+        def store_result(c, h):
+            lo, hi = CHUNKS[c]
+            nc.sync.dma_start(
+                out=out_0[h * GROUP:(h + 1) * GROUP, lo:hi].rearrange("(p t) m -> p t m", t=PACK), in_=result[c, h][:]
+            )
 
         def group_x(c):
             for g in range(GROUPS):
@@ -225,102 +255,146 @@ def tile_malware_excess_rounds_k1_kernel(tc, x, A, C, B_words, B_scales, S, keep
             for g in range(GROUPS):
                 quantize_act(label, c, g)
 
-        def finish(c, h):
-            recover(c, h)
+        def group_y(c, h):
             group_act("y", c, h, result[c, h][:])
+
+        def finish(c, h, slots=range(PACK)):
+            recover(c, h, slots)
+            store_result(c, h)
 
         on_vector, on_scalar = nc.vector.tensor_copy, nc.scalar.copy
 
-        group_weight(on_vector, "A", 0, 0)
+        keep_f32 = hold.tile([P, GROUPS, PACK], F32, align_bytes=64)
         group_x(0)
-        quantize_weight("A", 0, 0)
+        for h in range(GROUPS):
+            reorder_b_scales(h)
+        reorder_b_words(0)
+        group_weight(on_vector, "A", 0, 0)
+        group_weight(on_scalar, "A", 0, 1)
         quantize_both("x", 0)
+        quantize_weight("A", 0, 0)
         group_weight(on_vector, "A", 1, 0)
         group_weight(on_scalar, "A", 1, 1)
-        quantize_weight("A", 1, 0)
-        group_weight(on_scalar, "A", 0, 1)
-        quantize_weight("A", 1, 1)
-        round_one(0, 0)
-        quantize_weight("A", 0, 1)
         group_x(1)
-        add_x(nc.vector, 0, 0)
-        group_act("x1", 0, 0, state[0, 0][:])
-        group_weight(on_scalar, "C", 0, 0)
-        reorder_b(0)
-        round_one(0, 1)
+        nc.scalar.copy(out=keep_f32[:], in_=keep_raw[:])
+        quantize_weight("A", 0, 1)
+        quantize_weight("A", 1, 0)
+        multiply("A", "x", 0, 0)
+        quantize_weight("A", 1, 1)
+        multiply("A", "x", 0, 1)
+        reorder_b_words(1)
+        gate_one(0, 0)
         quantize_both("x", 1)
-        add_x(nc.vector, 0, 1)
-        group_act("x1", 0, 1, state[0, 1][:])
+        for h in range(GROUPS):
+            multiply("A", "x", 1, h)
+        gate_one(0, 1)
+        for h in range(GROUPS):
+            add_x(nc.vector, 0, h)
+        group_weight(on_scalar, "C", 0, 0)
+        for h in range(GROUPS):
+            group_act("x1", 0, h, state[0, h][:])
         group_weight(on_scalar, "C", 0, 1)
-        reorder_b(1)
+        gate_one(1, 0)
         quantize_weight("C", 0, 0)
+        add_x(nc.vector, 1, 0)
+        gate_one(1, 1)
         quantize_both("x1", 0)
+        add_x(nc.vector, 1, 1)
         group_weight(on_scalar, "C", 1, 0)
         group_x(2)
+        quantize_weight("C", 1, 0)
+        multiply("C", "x1", 0, 0)
         group_weight(on_vector, "C", 1, 1)
         quantize_weight("C", 0, 1)
-        round_one(1, 0)
         quantize_weight("C", 1, 1)
-        quantize_weight("C", 1, 0)
-        add_x(nc.vector, 1, 0)
-        group_act("x1", 1, 0, state[1, 0][:])
-        round_one(1, 1)
-        round_two(0, 0)
-        add_x(nc.vector, 1, 1)
-        group_act("x1", 1, 1, state[1, 1][:])
-        round_two(0, 1)
+        multiply("C", "x1", 0, 1)
         for h in range(GROUPS):
-            group_act("x2", 0, h, state[0, h][:])
+            group_act("x1", 1, h, state[1, h][:])
+        subtract_two(0, 0)
         quantize_both("x", 2)
+        for h in range(GROUPS):
+            multiply("A", "x", 2, h)
+        subtract_two(0, 1)
+        for h in range(GROUPS):
+            group_act("x2", 0, h, state[0, h][:], on_vector)
         quantize_both("x1", 1)
+        multiply("C", "x1", 1, 0)
         quantize_both("x2", 0)
 
         last = len(CHUNKS) - 1
+        shared, own = range(2, PACK), range(2)
+
+        def is_split(c):
+            return SPLIT and width(c) == 256 and 1 <= c <= last - 2
+
         for step in range(2, last + 1):
             first, second, third, fourth, ahead = step, step - 1, step - 2, step - 3, step + 1
+            rest = own if is_split(third) else range(PACK)
+            if is_split(third):
+                gate_three(third, 1, shared)
+                add_kept(third, 1, shared)
+            if fourth >= 0:
+                group_y(fourth, 1)
             if ahead <= last:
                 group_x(ahead)
+            gate_one(first, 0)
+            add_x(nc.gpsimd, first, 0)
+            multiply("C", "x1", second, 1)
+            gate_one(first, 1)
+            add_x(nc.gpsimd, first, 1)
+            multiply("B", "x2", third, 0)
+            multiply("B", "x2", third, 1, rest)
             for h in range(GROUPS):
-                round_one(first, h)
-                add_x(nc.gpsimd, first, h)
+                subtract_two(second, h)
             for h in range(GROUPS):
-                round_two(second, h)
-            for h in range(GROUPS):
-                group_act("x1", first, h, state[first, h][:])
                 group_act("x2", second, h, state[second, h][:])
             for h in range(GROUPS):
-                round_three(third, h)
+                group_act("x1", first, h, state[first, h][:])
+            if is_split(second):
+                scale_by_keep(second, 1, shared)
+            gate_three(third, 0)
+            gate_three(third, 1, rest)
+            quantize_both("x2", second)
+            if is_split(second):
+                multiply("B", "x2", second, 1, shared)
+            if step == last:
+                scale_by_keep(second, 0, range(PACK))
+                multiply("B", "x2", second, 0)
             if ahead <= last:
                 quantize_both("x", ahead)
-            for h in range(GROUPS):
-                finish(third, h)
+                for h in range(GROUPS):
+                    multiply("A", "x", ahead, h)
+            finish(third, 0)
+            group_y(third, 0)
             if fourth >= 0:
-                for g in range(GROUPS):
-                    quantize_result(fourth, g)
-            if step < last:
-                quantize_both("x1", first)
-                quantize_both("x2", second)
-            else:
-                quantize_both("x2", second)
-                quantize_both("x1", first)
+                quantize_result(fourth)
+            finish(third, 1, rest)
+            quantize_both("x1", first)
+            multiply("C", "x1", first, 0)
 
-        for g in range(GROUPS):
-            quantize_result(last - 2, g)
-        store_scales(0, CHUNKS[last - 2][1])
-        round_three(last - 1, 0)
+        multiply("C", "x1", last, 1)
+        multiply("B", "x2", last - 1, 1)
+        group_y(last - 2, 1)
+        gate_three(last - 1, 0)
+        add_kept(last - 1, 0, range(PACK))
+        store_result(last - 1, 0)
         for h in range(GROUPS):
-            round_two(last, h)
+            subtract_two(last, h)
             group_act("x2", last, h, state[last, h][:])
-        round_three(last - 1, 1)
+        group_y(last - 1, 0)
+        gate_three(last - 1, 1)
         quantize_both("x2", last)
         for h in range(GROUPS):
-            finish(last - 1, h)
-        round_three(last, 0)
-        round_three(last, 1)
-        finish(last, 0)
-        quantize_result(last - 1, 0)
-        finish(last, 1)
-        quantize_result(last - 1, 1)
-        for g in range(GROUPS):
-            quantize_result(last, g)
+            multiply("B", "x2", last, h)
+        finish(last - 1, 1)
+        group_y(last - 1, 1)
+        quantize_result(last - 2)
+        store_scales(0, CHUNKS[last - 2][1])
+        gate_three(last, 0)
+        gate_three(last, 1)
+        for h in range(GROUPS):
+            finish(last, h)
+            group_y(last, h)
+        quantize_result(last - 1)
+        quantize_result(last)
         store_scales(CHUNKS[last - 1][0], M)

@@ -20,10 +20,10 @@ GROUP = P * PACK
 GROUPS = N // GROUP
 BANK = 512
 FP4_N = 128
-SPLIT = True
+SPLIT = 1
 
 CHUNKS = [(0, 128), (128, 384), (384, 640), (640, 896), (896, 1152), (1152, 1408), (1408, 1536)]
-BLOCKS = [(0, 128), (128, 384), (384, 896), (896, 1536)]
+BLOCKS = CHUNKS
 
 
 def tile_malware_excess_rounds_k1_kernel(tc, x, A, C, B_words, B_scales, S, keep, out_0, out_1, out_2):
@@ -53,7 +53,7 @@ def tile_malware_excess_rounds_k1_kernel(tc, x, A, C, B_words, B_scales, S, keep
         def chunk_of(store, c, g):
             lo, hi = CHUNKS[c]
             b = max(i for i in range(len(BLOCKS)) if BLOCKS[i][0] <= lo)
-            return store[b, g][:, :, lo - BLOCKS[b][0]:hi - BLOCKS[b][0]]
+            return store[b, g][:]
 
         def load_weight_piece(src, label, g, h):
             raw_w[label, g, h] = load_rows(src, "%s%d_%d" % (label, g, h), g, h * GROUP, (h + 1) * GROUP)
@@ -69,19 +69,26 @@ def tile_malware_excess_rounds_k1_kernel(tc, x, A, C, B_words, B_scales, S, keep
         keep_raw = hold.tile([P, GROUPS, PACK], BF16, align_bytes=64)
         b_scale_raw = hold.tile([P, GROUPS, N], U8, align_bytes=64)
         nc.vector.memset(b_scale_raw[:].bitcast(I32), 0)
-        b_word_raw = hold.tile([P, GROUPS, 2 * N], U8, align_bytes=64)
-        nc.sync.dma_start(out=b_word_raw[:].bitcast(I32), in_=B_words.rearrange("g p n -> p g n").bitcast(I32))
+        b_word_raw = {}
+
+        def load_b_words(g):
+            raw = hold.tile([P, 2 * N], U8, name="B_raw%d" % g, align_bytes=64)
+            nc.sync.dma_start(out=raw[:].bitcast(I32), in_=B_words[g].bitcast(I32))
+            b_word_raw[g] = raw
+
+        load_b_words(0)
+        load_block(raw_x, x, "x", 0)
+        load_b_words(1)
+        load_weight_rows(A, "A", 0)
         for q in range(4):
             nc.sync.dma_start(
                 out=b_scale_raw[32 * q:32 * q + 4, :, :].bitcast(I32),
                 in_=B_scales[:, 4 * q:4 * q + 4, :].rearrange("g r n -> r g n").bitcast(I32),
             )
-        load_block(raw_x, x, "x", 0)
-        load_weight_rows(A, "A", 0)
         load_weight_rows(A, "A", 1)
+        load_block(raw_x, x, "x", 1)
         load_block(raw_s, S, "s", 0)
         nc.sync.dma_start(out=keep_raw[:], in_=keep.rearrange("(g p t) -> p g t", g=GROUPS, t=PACK))
-        load_block(raw_x, x, "x", 1)
         load_weight_rows(C, "C", 0)
         load_block(raw_s, S, "s", 1)
         load_weight_rows(C, "C", 1)
@@ -107,21 +114,16 @@ def tile_malware_excess_rounds_k1_kernel(tc, x, A, C, B_words, B_scales, S, keep
                 cols = slice(t * P, (t + 1) * P)
                 weights[label, g, h, t] = (codes[:, cols].bitcast(FP8X4), scales[:, cols])
 
-        b_scales = {}
+        b_words = {}
 
-        def reorder_b_words(h):
-            for g in range(GROUPS):
+        def reorder_b_words(g):
+            for h in range(GROUPS):
                 words = hold.tile([P, 2 * GROUP], U8, name="B_codes%d_%d" % (g, h), align_bytes=64)
                 nc.vector.tensor_copy(
                     out=words[:].rearrange("p (t c i b) -> p c t i b", t=PACK, i=8, b=2),
-                    in_=b_word_raw[:, g, 2 * GROUP * h:2 * GROUP * (h + 1)].rearrange("p (c i t b) -> p c t i b", i=8, t=PACK, b=2),
+                    in_=b_word_raw[g][:, 2 * GROUP * h:2 * GROUP * (h + 1)].rearrange("p (c i t b) -> p c t i b", i=8, t=PACK, b=2),
                 )
-                scales = b_scales[g, h]
-                for t in range(PACK):
-                    weights["B", g, h, t] = (
-                        words[:, 2 * P * t:2 * P * (t + 1)].bitcast(FP4X4),
-                        scales[:, P * t:P * (t + 1)],
-                    )
+                b_words[g, h] = words
 
         def reorder_b_scales(h):
             for g in range(GROUPS):
@@ -130,7 +132,11 @@ def tile_malware_excess_rounds_k1_kernel(tc, x, A, C, B_words, B_scales, S, keep
                     out=scales[:].rearrange("p (t c i) -> p c t i", t=PACK, i=16),
                     in_=b_scale_raw[:, g, GROUP * h:GROUP * (h + 1)].rearrange("p (c i t) -> p c t i", i=16, t=PACK),
                 )
-                b_scales[g, h] = scales
+                for t in range(PACK):
+                    weights["B", g, h, t] = (
+                        b_words[g, h][:, 2 * P * t:2 * P * (t + 1)].bitcast(FP4X4),
+                        scales[:, P * t:P * (t + 1)],
+                    )
 
         grouped_a, acts, state, result = {}, {}, {}, {}
         y_scales = hold.tile([P, GROUPS, M], U8, align_bytes=64)
@@ -265,13 +271,12 @@ def tile_malware_excess_rounds_k1_kernel(tc, x, A, C, B_words, B_scales, S, keep
         on_vector, on_scalar = nc.vector.tensor_copy, nc.scalar.copy
 
         keep_f32 = hold.tile([P, GROUPS, PACK], F32, align_bytes=64)
+        for g in range(GROUPS):
+            reorder_b_words(g)
         group_x(0)
-        for h in range(GROUPS):
-            reorder_b_scales(h)
-        reorder_b_words(0)
+        quantize_both("x", 0)
         group_weight(on_vector, "A", 0, 0)
         group_weight(on_scalar, "A", 0, 1)
-        quantize_both("x", 0)
         quantize_weight("A", 0, 0)
         group_weight(on_vector, "A", 1, 0)
         group_weight(on_scalar, "A", 1, 1)
@@ -280,41 +285,40 @@ def tile_malware_excess_rounds_k1_kernel(tc, x, A, C, B_words, B_scales, S, keep
         quantize_weight("A", 0, 1)
         quantize_weight("A", 1, 0)
         multiply("A", "x", 0, 0)
+        reorder_b_scales(0)
         quantize_weight("A", 1, 1)
         multiply("A", "x", 0, 1)
-        reorder_b_words(1)
-        gate_one(0, 0)
+        reorder_b_scales(1)
         quantize_both("x", 1)
         for h in range(GROUPS):
             multiply("A", "x", 1, h)
-        gate_one(0, 1)
         for h in range(GROUPS):
-            add_x(nc.vector, 0, h)
-        group_weight(on_scalar, "C", 0, 0)
+            gate_one(0, h)
+            add_x(nc.gpsimd, 0, h)
+        for h in range(GROUPS):
+            gate_one(1, h)
+        for h in range(GROUPS):
+            group_weight(on_scalar, "C", 0, h)
         for h in range(GROUPS):
             group_act("x1", 0, h, state[0, h][:])
-        group_weight(on_scalar, "C", 0, 1)
-        gate_one(1, 0)
-        quantize_weight("C", 0, 0)
-        add_x(nc.vector, 1, 0)
-        gate_one(1, 1)
-        quantize_both("x1", 0)
-        add_x(nc.vector, 1, 1)
         group_weight(on_scalar, "C", 1, 0)
-        group_x(2)
-        quantize_weight("C", 1, 0)
-        multiply("C", "x1", 0, 0)
+        for h in range(GROUPS):
+            add_x(nc.vector, 1, h)
+            quantize_weight("C", 0, h)
         group_weight(on_vector, "C", 1, 1)
-        quantize_weight("C", 0, 1)
+        quantize_both("x1", 0)
         quantize_weight("C", 1, 1)
         multiply("C", "x1", 0, 1)
+        quantize_weight("C", 1, 0)
+        multiply("C", "x1", 0, 0)
+        group_x(2)
         for h in range(GROUPS):
             group_act("x1", 1, h, state[1, h][:])
-        subtract_two(0, 0)
         quantize_both("x", 2)
         for h in range(GROUPS):
             multiply("A", "x", 2, h)
         subtract_two(0, 1)
+        subtract_two(0, 0)
         for h in range(GROUPS):
             group_act("x2", 0, h, state[0, h][:], on_vector)
         quantize_both("x1", 1)
@@ -325,7 +329,7 @@ def tile_malware_excess_rounds_k1_kernel(tc, x, A, C, B_words, B_scales, S, keep
         shared, own = range(2, PACK), range(2)
 
         def is_split(c):
-            return SPLIT and width(c) == 256 and 1 <= c <= last - 2
+            return SPLIT <= c <= last - 2
 
         for step in range(2, last + 1):
             first, second, third, fourth, ahead = step, step - 1, step - 2, step - 3, step + 1
@@ -368,6 +372,8 @@ def tile_malware_excess_rounds_k1_kernel(tc, x, A, C, B_words, B_scales, S, keep
             group_y(third, 0)
             if fourth >= 0:
                 quantize_result(fourth)
+            if step == last:
+                store_scales(0, CHUNKS[fourth][1])
             finish(third, 1, rest)
             quantize_both("x1", first)
             multiply("C", "x1", first, 0)
@@ -389,7 +395,6 @@ def tile_malware_excess_rounds_k1_kernel(tc, x, A, C, B_words, B_scales, S, keep
         finish(last - 1, 1)
         group_y(last - 1, 1)
         quantize_result(last - 2)
-        store_scales(0, CHUNKS[last - 2][1])
         gate_three(last, 0)
         gate_three(last, 1)
         for h in range(GROUPS):
@@ -397,4 +402,4 @@ def tile_malware_excess_rounds_k1_kernel(tc, x, A, C, B_words, B_scales, S, keep
             group_y(last, h)
         quantize_result(last - 1)
         quantize_result(last)
-        store_scales(CHUNKS[last - 1][0], M)
+        store_scales(CHUNKS[last - 2][0], M)

from contextlib import ExitStack

import concourse.mybir as mybir

N, M = 1024, 1536
FLOPS = 3 * 2 * N * N * M

F32 = mybir.dt.float32
BF16 = mybir.dt.bfloat16
I32 = mybir.dt.int32
U32 = mybir.dt.uint32
U8 = mybir.dt.uint8
FP8X4 = mybir.dt.float8_e4m3fn_x4
FP4X4 = mybir.dt.float4_e2m1fn_x4
ALU = mybir.AluOpType

P = 128
PACK = 4
GROUP = P * PACK
GROUPS = N // GROUP
BANK = 512
FP4_N = 128
SPLIT = 1

CHUNKS = [(0, 128), (128, 384), (384, 640), (640, 896), (896, 1152), (1152, 1408), (1408, 1536)]
BLOCKS = CHUNKS


def tile_malware_excess_rounds_k1_kernel(tc, x, A, C, B_words, B_scales, S, keep, out_0, out_1, out_2):
    nc = tc.nc
    with ExitStack() as ctx:
        hold = ctx.enter_context(tc.tile_pool(name="hold", bufs=1))
        work = ctx.enter_context(tc.tile_pool(name="work", bufs=2))
        psum = ctx.enter_context(tc.psum_pool(name="psum", bufs=8))
        ctx.enter_context(tc.manual_schedule())

        def load_rows(src, name, g, lo, hi):
            raw = hold.tile([P, PACK, hi - lo], BF16, name=name, align_bytes=64)
            rows = src[g * GROUP:(g + 1) * GROUP, lo:hi]
            nc.sync.dma_start(out=raw[:], in_=rows.rearrange("(p t) m -> p t m", t=PACK))
            return raw

        raw_x, raw_s, raw_w = {}, {}, {}

        def load_block(store, src, label, b):
            for g in range(GROUPS):
                store[b, g] = load_rows(src, "%s%d_%d" % (label, b, g), g, *BLOCKS[b])

        def load_weight(src, label, h):
            for g in range(GROUPS):
                raw_w[label, g, h] = load_rows(src, "%s%d_%d" % (label, g, h), g, h * GROUP, (h + 1) * GROUP)

        def chunk_of(store, c, g):
            lo, hi = CHUNKS[c]
            b = max(i for i in range(len(BLOCKS)) if BLOCKS[i][0] <= lo)
            return store[b, g][:]

        def load_weight_piece(src, label, g, h):
            raw_w[label, g, h] = load_rows(src, "%s%d_%d" % (label, g, h), g, h * GROUP, (h + 1) * GROUP)

        def load_half(store, src, label, b, g):
            store[b, g] = load_rows(src, "%s%d_%d" % (label, b, g), g, *BLOCKS[b])

        def load_weight_rows(src, label, g):
            raw = load_rows(src, "%s%d" % (label, g), g, 0, N)
            for h in range(GROUPS):
                raw_w[label, g, h] = raw[:, :, h * GROUP:(h + 1) * GROUP]

        keep_raw = hold.tile([P, GROUPS, PACK], BF16, align_bytes=64)
        b_scale_raw = hold.tile([P, GROUPS, N], U8, align_bytes=64)
        nc.vector.memset(b_scale_raw[:].bitcast(I32), 0)
        b_word_raw = {}

        def load_b_words(g):
            raw = hold.tile([P, 2 * N], U8, name="B_raw%d" % g, align_bytes=64)
            nc.sync.dma_start(out=raw[:].bitcast(I32), in_=B_words[g].bitcast(I32))
            b_word_raw[g] = raw

        load_b_words(0)
        load_block(raw_x, x, "x", 0)
        load_b_words(1)
        load_weight_rows(A, "A", 0)
        for q in range(4):
            nc.sync.dma_start(
                out=b_scale_raw[32 * q:32 * q + 4, :, :].bitcast(I32),
                in_=B_scales[:, 4 * q:4 * q + 4, :].rearrange("g r n -> r g n").bitcast(I32),
            )
        load_weight_rows(A, "A", 1)
        load_block(raw_x, x, "x", 1)
        load_block(raw_s, S, "s", 0)
        nc.sync.dma_start(out=keep_raw[:], in_=keep.rearrange("(g p t) -> p g t", g=GROUPS, t=PACK))
        load_weight_rows(C, "C", 0)
        load_block(raw_s, S, "s", 1)
        load_weight_rows(C, "C", 1)
        for b in range(2, len(BLOCKS)):
            load_block(raw_x, x, "x", b)
            load_block(raw_s, S, "s", b)

        grouped_w, weights = {}, {}

        def group_weight(copy, label, g, h):
            grouped = work.tile([P, GROUP * PACK], BF16, name="grouped_w", bufs=4, align_bytes=64)
            copy(
                out=grouped[:].rearrange("p (t c i j) -> p c t i j", t=PACK, i=2, j=PACK),
                in_=raw_w[label, g, h][:, :, :].rearrange("p j (c i t) -> p c t i j", i=2, t=PACK),
            )
            grouped_w[label, g, h] = grouped

        def quantize_weight(label, g, h):
            codes = hold.tile([P, GROUP], U32, name="%s_codes%d_%d" % (label, g, h), align_bytes=64)
            scales = hold.tile([P, GROUP], U8, name="%s_scales%d_%d" % (label, g, h), align_bytes=64)
            nc.vector.quantize_mx(out=codes[:].bitcast(FP8X4), scales=scales[:], in_=grouped_w[label, g, h][:])
            for t in range(PACK):
                cols = slice(t * P, (t + 1) * P)
                weights[label, g, h, t] = (codes[:, cols].bitcast(FP8X4), scales[:, cols])

        b_words = {}

        def reorder_b_words(g):
            for h in range(GROUPS):
                words = hold.tile([P, 2 * GROUP], U8, name="B_codes%d_%d" % (g, h), align_bytes=64)
                nc.vector.tensor_copy(
                    out=words[:].rearrange("p (t c i b) -> p c t i b", t=PACK, i=8, b=2),
                    in_=b_word_raw[g][:, 2 * GROUP * h:2 * GROUP * (h + 1)].rearrange("p (c i t b) -> p c t i b", i=8, t=PACK, b=2),
                )
                b_words[g, h] = words

        def reorder_b_scales(h):
            for g in range(GROUPS):
                scales = hold.tile([P, GROUP], U8, name="B_scales%d_%d" % (g, h), align_bytes=64)
                nc.vector.tensor_copy(
                    out=scales[:].rearrange("p (t c i) -> p c t i", t=PACK, i=16),
                    in_=b_scale_raw[:, g, GROUP * h:GROUP * (h + 1)].rearrange("p (c i t) -> p c t i", i=16, t=PACK),
                )
                for t in range(PACK):
                    weights["B", g, h, t] = (
                        b_words[g, h][:, 2 * P * t:2 * P * (t + 1)].bitcast(FP4X4),
                        scales[:, P * t:P * (t + 1)],
                    )

        grouped_a, acts, state, result = {}, {}, {}, {}
        y_scales = hold.tile([P, GROUPS, M], U8, align_bytes=64)

        def width(c):
            return CHUNKS[c][1] - CHUNKS[c][0]

        def group_act(label, c, g, src, copy=nc.scalar.copy):
            grouped = work.tile([P, width(c), PACK], BF16, name="grouped_%s%d" % (label, g), align_bytes=64)
            copy(
                out=grouped[:].rearrange("p (c i) t -> p c t i", i=4),
                in_=src.rearrange("p t (c i) -> p c t i", i=4),
            )
            grouped_a[label, c, g] = grouped

        def quantize_act(label, c, g):
            codes = work.tile([P, width(c)], U32, name="codes_%s%d" % (label, g), align_bytes=64)
            scales = work.tile([P, width(c)], U8, name="scales_%s%d" % (label, g), align_bytes=64)
            nc.vector.quantize_mx(
                out=codes[:].bitcast(FP8X4), scales=scales[:], in_=grouped_a[label, c, g][:].rearrange("p m t -> p (m t)")
            )
            acts[label, c, g] = (codes, scales)

        def quantize_result(c):
            lo, hi = CHUNKS[c]
            codes = work.tile([P, GROUPS, width(c)], U32, name="codes_y", bufs=3, align_bytes=64)
            for g in range(GROUPS):
                nc.vector.quantize_mx(
                    out=codes[:, g, :].bitcast(FP8X4), scales=y_scales[:, g, lo:hi],
                    in_=grouped_a["y", c, g][:].rearrange("p m t -> p (m t)"),
                )
            nc.sync.dma_start(
                out=out_1[:, :, lo:hi, :].rearrange("g p m t -> p g (m t)").bitcast(I32), in_=codes[:].bitcast(I32)
            )

        def store_scales(lo, hi):
            for q in range(4):
                nc.sync.dma_start(
                    out=out_2[:, 4 * q:4 * q + 4, lo:hi].rearrange("g r m -> r g m").bitcast(I32),
                    in_=y_scales[32 * q:32 * q + 4, :, lo:hi].bitcast(I32),
                )

        filled = {}

        def multiply(w_label, a_label, c, h, slots=range(PACK)):
            w = width(c)
            per_bank = BANK // w
            n = FP4_N if w_label == "B" else w
            for t0 in slots[::per_bank]:
                bank = psum.tile([P, per_bank, w], F32, name="bank")
                for t in range(t0, t0 + per_bank):
                    for m0 in range(0, w, n):
                        for g in range(GROUPS):
                            codes, scales = acts[a_label, c, g]
                            nc.tensor.matmul_mx(
                                out=bank[:, t - t0, m0:m0 + n],
                                lhsT=weights[w_label, g, h, t][0],
                                lhsT_scale=weights[w_label, g, h, t][1],
                                rhs=codes[:, m0:m0 + n].bitcast(FP8X4),
                                rhs_scale=scales[:, m0:m0 + n],
                                start=(g == 0),
                                stop=(g == GROUPS - 1),
                            )
                filled[w_label, c, h, t0] = bank

        def banks_of(w_label, c, h, slots=range(PACK)):
            per_bank = BANK // width(c)
            return [(filled[w_label, c, h, t0], slice(t0, t0 + per_bank)) for t0 in slots[::per_bank]]

        def gate_one(c, h):
            x1 = work.tile([P, PACK, width(c)], F32, name="state%d" % h, bufs=3, align_bytes=64)
            for bank, ts in banks_of("A", c, h):
                nc.vector.tensor_tensor(out=x1[:, ts, :], in0=bank[:], in1=chunk_of(raw_s, c, h)[:, ts, :], op=ALU.mult)
            state[c, h] = x1

        def add_x(engine, c, h):
            x1 = state[c, h]
            engine.tensor_tensor(out=x1[:], in0=x1[:], in1=chunk_of(raw_x, c, h), op=ALU.add)

        def subtract_two(c, h):
            x2 = state[c, h]
            for bank, ts in banks_of("C", c, h):
                nc.vector.tensor_tensor(out=x2[:, ts, :], in0=x2[:, ts, :], in1=bank[:], op=ALU.subtract)

        def gate_three(c, h, slots=range(PACK)):
            if (c, h) not in result:
                y = work.tile([P, PACK, width(c)], F32, name="result%d" % h, align_bytes=64)
                result[c, h] = y
            y = result[c, h]
            for bank, ts in banks_of("B", c, h, slots):
                nc.vector.tensor_tensor(out=y[:, ts, :], in0=bank[:], in1=chunk_of(raw_s, c, h)[:, ts, :], op=ALU.mult)

        def recover(c, h, slots):
            y = result[c, h]
            for t in slots:
                nc.vector.scalar_tensor_tensor(
                    out=y[:, t, :], in0=state[c, h][:, t, :], scalar=keep_f32[:, h, t:t + 1], in1=y[:, t, :],
                    op0=ALU.mult, op1=ALU.add,
                )

        def scale_by_keep(c, h, slots):
            for t in slots:
                x2 = state[c, h][:, t, :]
                nc.scalar.activation(out=x2, in_=x2, func=mybir.ActivationFunctionType.Copy, scale=keep_f32[:, h, t:t + 1])

        def add_kept(c, h, slots):
            ts = slice(slots.start, slots.stop)
            y = result[c, h][:, ts, :]
            nc.gpsimd.tensor_tensor(out=y, in0=y, in1=state[c, h][:, ts, :], op=ALU.add)

        def store_result(c, h):
            lo, hi = CHUNKS[c]
            nc.sync.dma_start(
                out=out_0[h * GROUP:(h + 1) * GROUP, lo:hi].rearrange("(p t) m -> p t m", t=PACK), in_=result[c, h][:]
            )

        def group_x(c):
            for g in range(GROUPS):
                group_act("x", c, g, chunk_of(raw_x, c, g))

        def quantize_both(label, c):
            for g in range(GROUPS):
                quantize_act(label, c, g)

        def group_y(c, h):
            group_act("y", c, h, result[c, h][:])

        def finish(c, h, slots=range(PACK)):
            recover(c, h, slots)
            store_result(c, h)

        on_vector, on_scalar = nc.vector.tensor_copy, nc.scalar.copy

        keep_f32 = hold.tile([P, GROUPS, PACK], F32, align_bytes=64)
        for g in range(GROUPS):
            reorder_b_words(g)
        group_x(0)
        quantize_both("x", 0)
        group_weight(on_vector, "A", 0, 0)
        group_weight(on_scalar, "A", 0, 1)
        quantize_weight("A", 0, 0)
        group_weight(on_vector, "A", 1, 0)
        group_weight(on_scalar, "A", 1, 1)
        group_x(1)
        nc.scalar.copy(out=keep_f32[:], in_=keep_raw[:])
        quantize_weight("A", 0, 1)
        quantize_weight("A", 1, 0)
        multiply("A", "x", 0, 0)
        reorder_b_scales(0)
        quantize_weight("A", 1, 1)
        multiply("A", "x", 0, 1)
        reorder_b_scales(1)
        quantize_both("x", 1)
        for h in range(GROUPS):
            multiply("A", "x", 1, h)
        for h in range(GROUPS):
            gate_one(0, h)
            add_x(nc.gpsimd, 0, h)
        for h in range(GROUPS):
            gate_one(1, h)
        for h in range(GROUPS):
            group_weight(on_scalar, "C", 0, h)
        for h in range(GROUPS):
            group_act("x1", 0, h, state[0, h][:])
        group_weight(on_scalar, "C", 1, 0)
        for h in range(GROUPS):
            add_x(nc.vector, 1, h)
            quantize_weight("C", 0, h)
        group_weight(on_vector, "C", 1, 1)
        quantize_both("x1", 0)
        quantize_weight("C", 1, 1)
        multiply("C", "x1", 0, 1)
        quantize_weight("C", 1, 0)
        multiply("C", "x1", 0, 0)
        group_x(2)
        for h in range(GROUPS):
            group_act("x1", 1, h, state[1, h][:])
        quantize_both("x", 2)
        for h in range(GROUPS):
            multiply("A", "x", 2, h)
        subtract_two(0, 1)
        subtract_two(0, 0)
        for h in range(GROUPS):
            group_act("x2", 0, h, state[0, h][:], on_vector)
        quantize_both("x1", 1)
        multiply("C", "x1", 1, 0)
        quantize_both("x2", 0)

        last = len(CHUNKS) - 1
        shared, own = range(2, PACK), range(2)

        def is_split(c):
            return SPLIT <= c <= last - 2

        for step in range(2, last + 1):
            first, second, third, fourth, ahead = step, step - 1, step - 2, step - 3, step + 1
            rest = own if is_split(third) else range(PACK)
            if is_split(third):
                gate_three(third, 1, shared)
                add_kept(third, 1, shared)
            if fourth >= 0:
                group_y(fourth, 1)
            if ahead <= last:
                group_x(ahead)
            gate_one(first, 0)
            add_x(nc.gpsimd, first, 0)
            multiply("C", "x1", second, 1)
            gate_one(first, 1)
            add_x(nc.gpsimd, first, 1)
            multiply("B", "x2", third, 0)
            multiply("B", "x2", third, 1, rest)
            for h in range(GROUPS):
                subtract_two(second, h)
            for h in range(GROUPS):
                group_act("x2", second, h, state[second, h][:])
            for h in range(GROUPS):
                group_act("x1", first, h, state[first, h][:])
            if is_split(second):
                scale_by_keep(second, 1, shared)
            gate_three(third, 0)
            gate_three(third, 1, rest)
            quantize_both("x2", second)
            if is_split(second):
                multiply("B", "x2", second, 1, shared)
            if step == last:
                scale_by_keep(second, 0, range(PACK))
                multiply("B", "x2", second, 0)
            if ahead <= last:
                quantize_both("x", ahead)
                for h in range(GROUPS):
                    multiply("A", "x", ahead, h)
            finish(third, 0)
            group_y(third, 0)
            if fourth >= 0:
                quantize_result(fourth)
            if step == last:
                store_scales(0, CHUNKS[fourth][1])
            finish(third, 1, rest)
            quantize_both("x1", first)
            multiply("C", "x1", first, 0)

        multiply("C", "x1", last, 1)
        multiply("B", "x2", last - 1, 1)
        group_y(last - 2, 1)
        gate_three(last - 1, 0)
        add_kept(last - 1, 0, range(PACK))
        store_result(last - 1, 0)
        for h in range(GROUPS):
            subtract_two(last, h)
            group_act("x2", last, h, state[last, h][:])
        group_y(last - 1, 0)
        gate_three(last - 1, 1)
        quantize_both("x2", last)
        for h in range(GROUPS):
            multiply("B", "x2", last, h)
        finish(last - 1, 1)
        group_y(last - 1, 1)
        quantize_result(last - 2)
        gate_three(last, 0)
        gate_three(last, 1)
        for h in range(GROUPS):
            finish(last, h)
            group_y(last, h)
        quantize_result(last - 1)
        quantize_result(last)
        store_scales(CHUNKS[last - 2][0], M)
